import numpy as np
CORES = [1,2,5,6,9,10,13,14,17,18,21,22,25,26,29,30]
N = 16
G1 = [0,1,2,3,4,5,6,7,8,9,10,11,12,13,14,15]
G2 = [0,1,2,3,4,5,6,7]
def setup_inputs(rng):
    return {"x1": rng.standard_normal((N, 128, 512), dtype=np.float32), "x2": rng.standard_normal((N, 128, 16), dtype=np.float32)}
def reference(x1, x2):
    out = {}
    y = np.full((N, 128, 512), np.nan, x1.dtype)
    s = x1[G1].sum(axis=0, dtype=np.float64).astype(x1.dtype)
    for r in G1:
        y[r] = s
    out["y1"] = y
    y = np.full((N, 128, 16), np.nan, x2.dtype)
    for i, r in enumerate(G2):
        y[r] = np.concatenate([x2[s][:, 2 * i:2 * i + 2] for s in G2], axis=1)
    out["y2"] = y
    return out

@@ -1,0 +1,217 @@
+from concourse.bass import DstId, RemoteDMATransfer
+
+NP = 4
+
+SCRATCH = {
+    "xs": ("dram", [NP, 128, 128], "float32"),
+    "r1": ("dram", [4, 128, 128], "float32"),
+    "r2": ("dram", [4, 128, 128], "float32"),
+    "res": ("dram", [NP, 128, 128], "float32"),
+    "all2": ("dram", [8, 128, 16], "float32"),
+}
+SEMAPHORES = ["ld1", "ld2", "a1", "a2", "a3", "snt", "e2", "l2", "st1", "pk"]
+
+
+def _bits(mask):
+    return [b for b in range(mask.bit_length()) if (mask >> b) & 1]
+
+
+def _mask(bits):
+    m = 0
+    for b in bits:
+        m |= 1 << b
+    return m
+
+
+def _plan(T, topo):
+    chips = sorted({topo.chip(c) for c in T.cores})
+    every = range((max(chips) + 1) * topo.CORES_PER_CHIP)
+    plan = {}
+    for ch in chips:
+        cs = [c for c in every if topo.chip(c) == ch]
+        ports = [c for c in cs if all(topo.may_write(c, d) for d in T.cores if d != c)]
+        spare = [c for c in cs if c not in T.cores]
+        pieces = []
+        for d in sorted({topo.die(c) for c in cs}):
+            first = [c for c in ports if topo.die(c) == d]
+            second = [c for c in spare if topo.die(c) == d]
+            pair = []
+            for sh in range(len(second)):
+                pair = [(p, second[(k + sh) % len(second)]) for k, p in enumerate(first)]
+                if all(p != h for p, h in pair):
+                    break
+            pieces += pair
+        plan[ch] = {"ranks": [c for c in T.cores if topo.chip(c) == ch], "pieces": pieces}
+    return chips, plan
+
+
+def _a2a_calls(T, topo):
+    mem = [T.cores[r] for r in T.tables["G2"]]
+    gate = [m for m in mem if all(topo.may_write(m, d) for d in mem if d != m)]
+    via = {}
+    for m in mem:
+        if m not in gate:
+            near = [w for w in gate if topo.chip(w) == topo.chip(m)]
+            same = [w for w in near if topo.die(w) == topo.die(m)]
+            via[m] = (same or near)[0]
+    calls = {}
+    for m in mem:
+        loc = [d for d in mem if d != m and topo.chip(d) == topo.chip(m)]
+        far = [d for d in mem if topo.chip(d) != topo.chip(m)]
+        on = _bits(topo.mask(m, loc[0]))
+        if m not in gate:
+            calls[m] = [(mem.index(m), loc, on, "e2")]
+            continue
+        off = _bits(topo.mask(m, far[0]))
+        slots = [m] + [p for p in mem if via.get(p) == m]
+        share = 1
+        while share * 2 * len(slots) <= len(off):
+            share *= 2
+        trs = [(mem.index(s), far, off[t * share:(t + 1) * share], "l2") for t, s in enumerate(slots)]
+        trs.append((mem.index(m), loc, [b for b in on if b not in off], "l2"))
+        calls[m] = trs
+    return mem, gate, calls
+
+
+def rank_program(g, core, T, topo):
+    chips, plan = _plan(T, topo)
+    ch = topo.chip(core)
+    if ch not in plan:
+        return
+    S = T.sem
+    ranks, pieces = plan[ch]["ranks"], plan[ch]["pieces"]
+    is_rank = core in ranks
+    mem, gate, calls = _a2a_calls(T, topo)
+    member = core in mem
+    sent = [0]
+
+    def dst(c):
+        rid, pid, _se = topo.addr(c)
+        return DstId(rid=rid, pnc=pid)
+
+    def fused(trs):
+        g.remote_dma_fused(trs, local_sem=S.snt)
+
+    def a2a_send():
+        trs = []
+        for slot, dsts, bits, sem in calls[core]:
+            trs.append(RemoteDMATransfer(dst_ids=[dst(d) for d in dsts], dma_engine_mask=_mask(bits),
+                                         remote_sem=S[sem], srcs=[T.all2[slot]],
+                                         dsts=[T.all2[slot] for _d in dsts], alu_op=0))
+            sent[0] += len(bits)
+        fused(trs)
+
+    def lands(sem):
+        n, slots = 0, []
+        for m in mem:
+            for slot, dsts, bits, s in calls[m]:
+                if s == sem and core in dsts:
+                    n += len(bits)
+                    slots.append(slot)
+        return n, slots
+
+    if is_rank:
+        g.sync.dma_start(T.xs[:], T.x1[:]).then_inc(S.ld1, 16)
+    if member:
+        me = mem.index(core)
+        g.scalar.dma_start(T.all2[me], T.x2[:]).then_inc(S.ld2, 16)
+
+    if is_rank:
+        k = ranks.index(core)
+        on = _bits(topo.mask(core, [c for c in ranks if c != core][0]))
+        w = len(on) // NP
+        g.wait_ge(S.ld1, 16)
+        trs = []
+        for q, (s1, _s2) in enumerate(pieces):
+            if s1 == core:
+                continue
+            trs.append(RemoteDMATransfer(dst_ids=[dst(s1)], dma_engine_mask=_mask(on[q * w:(q + 1) * w]),
+                                         remote_sem=S.a1, srcs=[T.xs[q]], dsts=[T.r1[k]], alu_op=0))
+            sent[0] += w
+        fused(trs)
+
+    if member and core not in gate:
+        g.wait_ge(S.ld2, 16)
+        a2a_send()
+
+    ci = chips.index(ch)
+    for q, (s1, s2) in enumerate(pieces):
+        if s1 != core:
+            continue
+        w = len(_bits(topo.mask(ranks[0], ranks[1]))) // NP
+        g.wait_ge(S.a1, w * len([r for r in ranks if r != core]))
+        srcs = [T.xs[q] if r == core else T.r1[j] for j, r in enumerate(ranks)]
+        far = [plan[c2]["pieces"][q][1] for c2 in chips if c2 != ch]
+        offm = topo.mask(core, s2)
+        for d in far:
+            offm &= topo.mask(core, d)
+        onm = topo.mask(core, s2) & ~offm
+        fused([
+            RemoteDMATransfer(dst_ids=[dst(d) for d in far], dma_engine_mask=offm, remote_sem=S.a2,
+                              srcs=srcs, dsts=[T.r2[ci] for _d in far], alu_op=1),
+            RemoteDMATransfer(dst_ids=[dst(s2)], dma_engine_mask=onm, remote_sem=S.a2,
+                              srcs=srcs, dsts=[T.r2[ci]], alu_op=1),
+        ])
+        sent[0] += len(_bits(offm)) + len(_bits(onm))
+
+    if member and core in gate:
+        g.wait_ge(S.ld2, 16)
+        n_e, _sl = lands("e2")
+        g.wait_ge(S.e2, n_e)
+        a2a_send()
+
+    for q, (s1, s2) in enumerate(pieces):
+        if s2 != core:
+            continue
+        n = 0
+        for c2 in chips:
+            p1 = plan[c2]["pieces"][q][0]
+            offm = topo.mask(p1, plan[c2]["pieces"][q][1])
+            for c3 in chips:
+                if c3 != c2:
+                    offm &= topo.mask(p1, plan[c3]["pieces"][q][1])
+            n += len(_bits(offm)) if c2 != ch else len(_bits(topo.mask(p1, s2) & ~offm))
+        g.wait_ge(S.a2, n)
+        m = topo.mask(core, ranks[0])
+        for r in ranks:
+            m &= topo.mask(core, r)
+        fused([RemoteDMATransfer(dst_ids=[dst(r) for r in ranks], dma_engine_mask=m, remote_sem=S.a3,
+                                 srcs=[T.r2[j] for j in range(len(chips))],
+                                 dsts=[T.res[q] for _r in ranks], alu_op=1)])
+        sent[0] += len(_bits(m))
+
+    npk = 0
+    if member:
+        bw = T.x2.shape[1] // len(mem)
+
+        def pick(queue, j):
+            src = T.x2 if j == me else T.all2[j]
+            queue.dma_start(T.y2[:, bw * j:bw * (j + 1)], src[:, bw * me:bw * (me + 1)]).then_inc(S.pk, 16)
+
+        n_e, early = lands("e2")
+        n_l, late = lands("l2")
+        g.scalar.wait_ge(S.e2, n_e)
+        for j in [me] + early:
+            pick(g.scalar, j)
+        g.scalar.wait_ge(S.l2, n_l)
+        g.sync.wait_ge(S.l2, n_l)
+        for t, j in enumerate(late):
+            pick(g.scalar if t % 2 == 0 else g.sync, j)
+        npk = 1 + len(early) + len(late)
+
+    if is_rank:
+        n = 0
+        for _s1, s2 in pieces:
+            m = topo.mask(s2, ranks[0])
+            for r in ranks:
+                m &= topo.mask(s2, r)
+            n += len(_bits(m))
+        g.sync.wait_ge(S.a3, n)
+        g.sync.dma_start(T.y1[:], T.res[:]).then_inc(S.st1, 16)
+
+    if sent[0]:
+        g.wait_ge(S.snt, sent[0])
+    if npk:
+        g.wait_ge(S.pk, 16 * npk)
+    if is_rank:
+        g.wait_ge(S.st1, 16)

@@ -1,15 +1,19 @@
 from concourse.bass import DstId, RemoteDMATransfer
 
 NP = 4
+NC = 2
+PW = 128 // NC
+XR = 128 // NC
 
 SCRATCH = {
-    "xs": ("dram", [NP, 128, 128], "float32"),
-    "r1": ("dram", [4, 128, 128], "float32"),
-    "r2": ("dram", [4, 128, 128], "float32"),
-    "res": ("dram", [NP, 128, 128], "float32"),
+    "xs": ("dram", [NC * NP, 128, PW], "float32"),
+    "r1": ("dram", [NC * 4, 128, PW], "float32"),
+    "r2": ("dram", [NC * 4, 128, PW], "float32"),
+    "res": ("dram", [NC * NP, 128, PW], "float32"),
     "all2": ("dram", [8, 128, 16], "float32"),
 }
-SEMAPHORES = ["ld1", "ld2", "a1", "a2", "a3", "snt", "e2", "l2", "st1", "pk"]
+SEMAPHORES = (["ld2", "snt", "e2", "l2", "st1", "pk"]
+              + ["%s_%d" % (n, c) for n in ("ld1", "a1", "a2", "a3") for c in range(NC)])
 
 
 def _bits(mask):
@@ -85,6 +89,9 @@ def rank_program(g, core, T, topo):
     member = core in mem
     sent = [0]
 
+    def sem(name, c):
+        return S["%s_%d" % (name, c)]
+
     def dst(c):
         rid, pid, _se = topo.addr(c)
         return DstId(rid=rid, pnc=pid)
@@ -94,41 +101,45 @@ def rank_program(g, core, T, topo):
 
     def a2a_send():
         trs = []
-        for slot, dsts, bits, sem in calls[core]:
+        for slot, dsts, bits, sm in calls[core]:
             trs.append(RemoteDMATransfer(dst_ids=[dst(d) for d in dsts], dma_engine_mask=_mask(bits),
-                                         remote_sem=S[sem], srcs=[T.all2[slot]],
+                                         remote_sem=S[sm], srcs=[T.all2[slot]],
                                          dsts=[T.all2[slot] for _d in dsts], alu_op=0))
             sent[0] += len(bits)
         fused(trs)
 
-    def lands(sem):
+    def lands(sm):
         n, slots = 0, []
         for m in mem:
             for slot, dsts, bits, s in calls[m]:
-                if s == sem and core in dsts:
+                if s == sm and core in dsts:
                     n += len(bits)
                     slots.append(slot)
         return n, slots
 
-    if is_rank:
-        g.sync.dma_start(T.xs[:], T.x1[:]).then_inc(S.ld1, 16)
     if member:
         me = mem.index(core)
         g.scalar.dma_start(T.all2[me], T.x2[:]).then_inc(S.ld2, 16)
+    if is_rank:
+        for c in range(NC):
+            queue = g.sync if c % 2 == 0 else g.scalar
+            queue.dma_start(T.xs[c * NP:(c + 1) * NP], T.x1[c * XR:(c + 1) * XR, :]).then_inc(sem("ld1", c), 16)
 
     if is_rank:
         k = ranks.index(core)
         on = _bits(topo.mask(core, [c for c in ranks if c != core][0]))
         w = len(on) // NP
-        g.wait_ge(S.ld1, 16)
-        trs = []
-        for q, (s1, _s2) in enumerate(pieces):
-            if s1 == core:
-                continue
-            trs.append(RemoteDMATransfer(dst_ids=[dst(s1)], dma_engine_mask=_mask(on[q * w:(q + 1) * w]),
-                                         remote_sem=S.a1, srcs=[T.xs[q]], dsts=[T.r1[k]], alu_op=0))
-            sent[0] += w
-        fused(trs)
+        for c in range(NC):
+            g.wait_ge(sem("ld1", c), 16)
+            trs = []
+            for q, (s1, _s2) in enumerate(pieces):
+                if s1 == core:
+                    continue
+                trs.append(RemoteDMATransfer(dst_ids=[dst(s1)], dma_engine_mask=_mask(on[q * w:(q + 1) * w]),
+                                             remote_sem=sem("a1", c), srcs=[T.xs[c * NP + q]],
+                                             dsts=[T.r1[c * 4 + k]], alu_op=0))
+                sent[0] += w
+            fused(trs)
 
     if member and core not in gate:
         g.wait_ge(S.ld2, 16)
@@ -139,20 +150,21 @@ def rank_program(g, core, T, topo):
         if s1 != core:
             continue
         w = len(_bits(topo.mask(ranks[0], ranks[1]))) // NP
-        g.wait_ge(S.a1, w * len([r for r in ranks if r != core]))
-        srcs = [T.xs[q] if r == core else T.r1[j] for j, r in enumerate(ranks)]
         far = [plan[c2]["pieces"][q][1] for c2 in chips if c2 != ch]
         offm = topo.mask(core, s2)
         for d in far:
             offm &= topo.mask(core, d)
         onm = topo.mask(core, s2) & ~offm
-        fused([
-            RemoteDMATransfer(dst_ids=[dst(d) for d in far], dma_engine_mask=offm, remote_sem=S.a2,
-                              srcs=srcs, dsts=[T.r2[ci] for _d in far], alu_op=1),
-            RemoteDMATransfer(dst_ids=[dst(s2)], dma_engine_mask=onm, remote_sem=S.a2,
-                              srcs=srcs, dsts=[T.r2[ci]], alu_op=1),
-        ])
-        sent[0] += len(_bits(offm)) + len(_bits(onm))
+        for c in range(NC):
+            g.wait_ge(sem("a1", c), w * len([r for r in ranks if r != core]))
+            srcs = [T.xs[c * NP + q] if r == core else T.r1[c * 4 + j] for j, r in enumerate(ranks)]
+            fused([
+                RemoteDMATransfer(dst_ids=[dst(d) for d in far], dma_engine_mask=offm, remote_sem=sem("a2", c),
+                                  srcs=srcs, dsts=[T.r2[c * 4 + ci] for _d in far], alu_op=1),
+                RemoteDMATransfer(dst_ids=[dst(s2)], dma_engine_mask=onm, remote_sem=sem("a2", c),
+                                  srcs=srcs, dsts=[T.r2[c * 4 + ci]], alu_op=1),
+            ])
+            sent[0] += len(_bits(offm)) + len(_bits(onm))
 
     if member and core in gate:
         g.wait_ge(S.ld2, 16)
@@ -171,14 +183,15 @@ def rank_program(g, core, T, topo):
                 if c3 != c2:
                     offm &= topo.mask(p1, plan[c3]["pieces"][q][1])
             n += len(_bits(offm)) if c2 != ch else len(_bits(topo.mask(p1, s2) & ~offm))
-        g.wait_ge(S.a2, n)
         m = topo.mask(core, ranks[0])
         for r in ranks:
             m &= topo.mask(core, r)
-        fused([RemoteDMATransfer(dst_ids=[dst(r) for r in ranks], dma_engine_mask=m, remote_sem=S.a3,
-                                 srcs=[T.r2[j] for j in range(len(chips))],
-                                 dsts=[T.res[q] for _r in ranks], alu_op=1)])
-        sent[0] += len(_bits(m))
+        for c in range(NC):
+            g.wait_ge(sem("a2", c), n)
+            fused([RemoteDMATransfer(dst_ids=[dst(r) for r in ranks], dma_engine_mask=m, remote_sem=sem("a3", c),
+                                     srcs=[T.r2[c * 4 + j] for j in range(len(chips))],
+                                     dsts=[T.res[c * NP + q] for _r in ranks], alu_op=1)])
+            sent[0] += len(_bits(m))
 
     npk = 0
     if member:
@@ -206,12 +219,13 @@ def rank_program(g, core, T, topo):
             for r in ranks:
                 m &= topo.mask(s2, r)
             n += len(_bits(m))
-        g.sync.wait_ge(S.a3, n)
-        g.sync.dma_start(T.y1[:], T.res[:]).then_inc(S.st1, 16)
+        for c in range(NC):
+            g.sync.wait_ge(sem("a3", c), n)
+            g.sync.dma_start(T.y1[c * XR:(c + 1) * XR, :], T.res[c * NP:(c + 1) * NP]).then_inc(S.st1, 16)
 
     if sent[0]:
         g.wait_ge(S.snt, sent[0])
     if npk:
         g.wait_ge(S.pk, 16 * npk)
     if is_rank:
-        g.wait_ge(S.st1, 16)
+        g.wait_ge(S.st1, 16 * NC)

@@ -1,7 +1,7 @@
 from concourse.bass import DstId, RemoteDMATransfer
 
 NP = 4
-NC = 2
+NC = 4
 PW = 128 // NC
 XR = 128 // NC
 
@@ -117,13 +117,13 @@ def rank_program(g, core, T, topo):
                     slots.append(slot)
         return n, slots
 
-    if member:
-        me = mem.index(core)
-        g.scalar.dma_start(T.all2[me], T.x2[:]).then_inc(S.ld2, 16)
     if is_rank:
         for c in range(NC):
             queue = g.sync if c % 2 == 0 else g.scalar
             queue.dma_start(T.xs[c * NP:(c + 1) * NP], T.x1[c * XR:(c + 1) * XR, :]).then_inc(sem("ld1", c), 16)
+    if member:
+        me = mem.index(core)
+        g.scalar.dma_start(T.all2[me], T.x2[:]).then_inc(S.ld2, 16)
 
     if is_rank:
         k = ranks.index(core)

from concourse.bass import DstId, RemoteDMATransfer

NP = 4
NC = 4
PW = 128 // NC
XR = 128 // NC

SCRATCH = {
    "xs": ("dram", [NC * NP, 128, PW], "float32"),
    "r1": ("dram", [NC * 4, 128, PW], "float32"),
    "r2": ("dram", [NC * 4, 128, PW], "float32"),
    "res": ("dram", [NC * NP, 128, PW], "float32"),
    "all2": ("dram", [8, 128, 16], "float32"),
}
SEMAPHORES = (["ld2", "snt", "e2", "l2", "st1", "pk"]
              + ["%s_%d" % (n, c) for n in ("ld1", "a1", "a2", "a3") for c in range(NC)])


def _bits(mask):
    return [b for b in range(mask.bit_length()) if (mask >> b) & 1]


def _mask(bits):
    m = 0
    for b in bits:
        m |= 1 << b
    return m


def _plan(T, topo):
    chips = sorted({topo.chip(c) for c in T.cores})
    every = range((max(chips) + 1) * topo.CORES_PER_CHIP)
    plan = {}
    for ch in chips:
        cs = [c for c in every if topo.chip(c) == ch]
        ports = [c for c in cs if all(topo.may_write(c, d) for d in T.cores if d != c)]
        spare = [c for c in cs if c not in T.cores]
        pieces = []
        for d in sorted({topo.die(c) for c in cs}):
            first = [c for c in ports if topo.die(c) == d]
            second = [c for c in spare if topo.die(c) == d]
            pair = []
            for sh in range(len(second)):
                pair = [(p, second[(k + sh) % len(second)]) for k, p in enumerate(first)]
                if all(p != h for p, h in pair):
                    break
            pieces += pair
        plan[ch] = {"ranks": [c for c in T.cores if topo.chip(c) == ch], "pieces": pieces}
    return chips, plan


def _a2a_calls(T, topo):
    mem = [T.cores[r] for r in T.tables["G2"]]
    gate = [m for m in mem if all(topo.may_write(m, d) for d in mem if d != m)]
    via = {}
    for m in mem:
        if m not in gate:
            near = [w for w in gate if topo.chip(w) == topo.chip(m)]
            same = [w for w in near if topo.die(w) == topo.die(m)]
            via[m] = (same or near)[0]
    calls = {}
    for m in mem:
        loc = [d for d in mem if d != m and topo.chip(d) == topo.chip(m)]
        far = [d for d in mem if topo.chip(d) != topo.chip(m)]
        on = _bits(topo.mask(m, loc[0]))
        if m not in gate:
            calls[m] = [(mem.index(m), loc, on, "e2")]
            continue
        off = _bits(topo.mask(m, far[0]))
        slots = [m] + [p for p in mem if via.get(p) == m]
        share = 1
        while share * 2 * len(slots) <= len(off):
            share *= 2
        trs = [(mem.index(s), far, off[t * share:(t + 1) * share], "l2") for t, s in enumerate(slots)]
        trs.append((mem.index(m), loc, [b for b in on if b not in off], "l2"))
        calls[m] = trs
    return mem, gate, calls


def rank_program(g, core, T, topo):
    chips, plan = _plan(T, topo)
    ch = topo.chip(core)
    if ch not in plan:
        return
    S = T.sem
    ranks, pieces = plan[ch]["ranks"], plan[ch]["pieces"]
    is_rank = core in ranks
    mem, gate, calls = _a2a_calls(T, topo)
    member = core in mem
    sent = [0]

    def sem(name, c):
        return S["%s_%d" % (name, c)]

    def dst(c):
        rid, pid, _se = topo.addr(c)
        return DstId(rid=rid, pnc=pid)

    def fused(trs):
        g.remote_dma_fused(trs, local_sem=S.snt)

    def a2a_send():
        trs = []
        for slot, dsts, bits, sm in calls[core]:
            trs.append(RemoteDMATransfer(dst_ids=[dst(d) for d in dsts], dma_engine_mask=_mask(bits),
                                         remote_sem=S[sm], srcs=[T.all2[slot]],
                                         dsts=[T.all2[slot] for _d in dsts], alu_op=0))
            sent[0] += len(bits)
        fused(trs)

    def lands(sm):
        n, slots = 0, []
        for m in mem:
            for slot, dsts, bits, s in calls[m]:
                if s == sm and core in dsts:
                    n += len(bits)
                    slots.append(slot)
        return n, slots

    if is_rank:
        for c in range(NC):
            queue = g.sync if c % 2 == 0 else g.scalar
            queue.dma_start(T.xs[c * NP:(c + 1) * NP], T.x1[c * XR:(c + 1) * XR, :]).then_inc(sem("ld1", c), 16)
    if member:
        me = mem.index(core)
        g.scalar.dma_start(T.all2[me], T.x2[:]).then_inc(S.ld2, 16)

    if is_rank:
        k = ranks.index(core)
        on = _bits(topo.mask(core, [c for c in ranks if c != core][0]))
        w = len(on) // NP
        for c in range(NC):
            g.wait_ge(sem("ld1", c), 16)
            trs = []
            for q, (s1, _s2) in enumerate(pieces):
                if s1 == core:
                    continue
                trs.append(RemoteDMATransfer(dst_ids=[dst(s1)], dma_engine_mask=_mask(on[q * w:(q + 1) * w]),
                                             remote_sem=sem("a1", c), srcs=[T.xs[c * NP + q]],
                                             dsts=[T.r1[c * 4 + k]], alu_op=0))
                sent[0] += w
            fused(trs)

    if member and core not in gate:
        g.wait_ge(S.ld2, 16)
        a2a_send()

    ci = chips.index(ch)
    for q, (s1, s2) in enumerate(pieces):
        if s1 != core:
            continue
        w = len(_bits(topo.mask(ranks[0], ranks[1]))) // NP
        far = [plan[c2]["pieces"][q][1] for c2 in chips if c2 != ch]
        offm = topo.mask(core, s2)
        for d in far:
            offm &= topo.mask(core, d)
        onm = topo.mask(core, s2) & ~offm
        for c in range(NC):
            g.wait_ge(sem("a1", c), w * len([r for r in ranks if r != core]))
            srcs = [T.xs[c * NP + q] if r == core else T.r1[c * 4 + j] for j, r in enumerate(ranks)]
            fused([
                RemoteDMATransfer(dst_ids=[dst(d) for d in far], dma_engine_mask=offm, remote_sem=sem("a2", c),
                                  srcs=srcs, dsts=[T.r2[c * 4 + ci] for _d in far], alu_op=1),
                RemoteDMATransfer(dst_ids=[dst(s2)], dma_engine_mask=onm, remote_sem=sem("a2", c),
                                  srcs=srcs, dsts=[T.r2[c * 4 + ci]], alu_op=1),
            ])
            sent[0] += len(_bits(offm)) + len(_bits(onm))

    if member and core in gate:
        g.wait_ge(S.ld2, 16)
        n_e, _sl = lands("e2")
        g.wait_ge(S.e2, n_e)
        a2a_send()

    for q, (s1, s2) in enumerate(pieces):
        if s2 != core:
            continue
        n = 0
        for c2 in chips:
            p1 = plan[c2]["pieces"][q][0]
            offm = topo.mask(p1, plan[c2]["pieces"][q][1])
            for c3 in chips:
                if c3 != c2:
                    offm &= topo.mask(p1, plan[c3]["pieces"][q][1])
            n += len(_bits(offm)) if c2 != ch else len(_bits(topo.mask(p1, s2) & ~offm))
        m = topo.mask(core, ranks[0])
        for r in ranks:
            m &= topo.mask(core, r)
        for c in range(NC):
            g.wait_ge(sem("a2", c), n)
            fused([RemoteDMATransfer(dst_ids=[dst(r) for r in ranks], dma_engine_mask=m, remote_sem=sem("a3", c),
                                     srcs=[T.r2[c * 4 + j] for j in range(len(chips))],
                                     dsts=[T.res[c * NP + q] for _r in ranks], alu_op=1)])
            sent[0] += len(_bits(m))

    npk = 0
    if member:
        bw = T.x2.shape[1] // len(mem)

        def pick(queue, j):
            src = T.x2 if j == me else T.all2[j]
            queue.dma_start(T.y2[:, bw * j:bw * (j + 1)], src[:, bw * me:bw * (me + 1)]).then_inc(S.pk, 16)

        n_e, early = lands("e2")
        n_l, late = lands("l2")
        g.scalar.wait_ge(S.e2, n_e)
        for j in [me] + early:
            pick(g.scalar, j)
        g.scalar.wait_ge(S.l2, n_l)
        g.sync.wait_ge(S.l2, n_l)
        for t, j in enumerate(late):
            pick(g.scalar if t % 2 == 0 else g.sync, j)
        npk = 1 + len(early) + len(late)

    if is_rank:
        n = 0
        for _s1, s2 in pieces:
            m = topo.mask(s2, ranks[0])
            for r in ranks:
                m &= topo.mask(s2, r)
            n += len(_bits(m))
        for c in range(NC):
            g.sync.wait_ge(sem("a3", c), n)
            g.sync.dma_start(T.y1[c * XR:(c + 1) * XR, :], T.res[c * NP:(c + 1) * NP]).then_inc(S.st1, 16)

    if sent[0]:
        g.wait_ge(S.snt, sent[0])
    if npk:
        g.wait_ge(S.pk, 16 * npk)
    if is_rank:
        g.wait_ge(S.st1, 16 * NC)
